import numpy as np
CORES = [2,10,18,26,34,42,50,58,66,74,82,90,98,106,114,122]
N = 16
GROUPS = [[0,2,4,6,8,10,12,14],[1,3,5,7,9,11,13,15]]
def setup_inputs(rng):
    return {"x": rng.standard_normal((N, 128, 128), dtype=np.float32)}
def reference(x):
    y = np.empty((N, 128, 128), x.dtype)
    for g in GROUPS:
        n = len(g); b = x.shape[2] // n
        for i, r in enumerate(g):
            y[r] = np.concatenate([x[s][:, i * b:(i + 1) * b] for s in g], axis=1)
    return {"y": y}

@@ -1,0 +1,38 @@
+from concourse.bass import DstId, RemoteDMATransfer
+
+SCRATCH = {
+    "xs": ("sbuf", [128, 128], "float32"),
+    "land": ("sbuf", [128, 128], "float32"),
+}
+SEMAPHORES = ["loaded", "sent", "arrived", "stored"]
+
+
+def rank_program(g, core, T, topo):
+    rank = T.rank_of(core)
+    if rank is None:
+        return
+    grp = [m for m in T.tables["GROUPS"] if rank in m][0]
+    n = len(grp)
+    i = grp.index(rank)
+    b = T.x.shape[1] // n
+
+    def blk(j):
+        return slice(j * b, (j + 1) * b)
+
+    g.sync.dma_start(T.xs[:, :], T.x[:, :]).then_inc(T.sem.loaded, 16)
+    g.scalar.dma_start(T.land[:, blk(i)], T.x[:, blk(i)]).then_inc(T.sem.arrived, 16)
+
+    g.wait_ge(T.sem.loaded, 16)
+    trs = []
+    for k in range(1, n):
+        j = (i + k) % n
+        rid, pid, _se = topo.addr(T.cores[grp[j]])
+        trs.append(RemoteDMATransfer(
+            dst_ids=[DstId(rid=rid, pnc=pid)], dma_engine_mask=1 << (k - 1), remote_sem=T.sem.arrived,
+            src=T.xs[:, blk(j)], dst=T.land[:, blk(i)]))
+    g.remote_dma_fused(trs, local_sem=T.sem.sent)
+
+    g.sync.wait_ge(T.sem.arrived, 16 + (n - 1))
+    g.sync.dma_start(T.y[:, :], T.land[:, :]).then_inc(T.sem.stored, 16)
+    g.wait_ge(T.sem.sent, n - 1)
+    g.sync.wait_ge(T.sem.stored, 16)

@@ -5,6 +5,7 @@ SCRATCH = {
     "land": ("sbuf", [128, 128], "float32"),
 }
 SEMAPHORES = ["loaded", "sent", "arrived", "stored"]
+CALLS = [(4, 2), (2, 4), (1, 8)]
 
 
 def rank_program(g, core, T, topo):
@@ -20,19 +21,24 @@ def rank_program(g, core, T, topo):
         return slice(j * b, (j + 1) * b)
 
     g.sync.dma_start(T.xs[:, :], T.x[:, :]).then_inc(T.sem.loaded, 16)
-    g.scalar.dma_start(T.land[:, blk(i)], T.x[:, blk(i)]).then_inc(T.sem.arrived, 16)
+    g.sync.dma_start(T.land[:, blk(i)], T.x[:, blk(i)]).then_inc(T.sem.arrived, 16)
 
     g.wait_ge(T.sem.loaded, 16)
-    trs = []
-    for k in range(1, n):
-        j = (i + k) % n
-        rid, pid, _se = topo.addr(T.cores[grp[j]])
-        trs.append(RemoteDMATransfer(
-            dst_ids=[DstId(rid=rid, pnc=pid)], dma_engine_mask=1 << (k - 1), remote_sem=T.sem.arrived,
-            src=T.xs[:, blk(j)], dst=T.land[:, blk(i)]))
-    g.remote_dma_fused(trs, local_sem=T.sem.sent)
+    k = 1
+    total = 0
+    for cnt, eng in CALLS:
+        trs = []
+        for q in range(cnt):
+            j = (i + k) % n
+            rid, pid, _se = topo.addr(T.cores[grp[j]])
+            trs.append(RemoteDMATransfer(
+                dst_ids=[DstId(rid=rid, pnc=pid)], dma_engine_mask=((1 << eng) - 1) << (q * eng),
+                remote_sem=T.sem.arrived, src=T.xs[:, blk(j)], dst=T.land[:, blk(i)]))
+            k += 1
+            total += eng
+        g.remote_dma_fused(trs, local_sem=T.sem.sent)
 
-    g.sync.wait_ge(T.sem.arrived, 16 + (n - 1))
+    g.sync.wait_ge(T.sem.arrived, 16 + total)
     g.sync.dma_start(T.y[:, :], T.land[:, :]).then_inc(T.sem.stored, 16)
-    g.wait_ge(T.sem.sent, n - 1)
+    g.wait_ge(T.sem.sent, total)
     g.sync.wait_ge(T.sem.stored, 16)

@@ -1,11 +1,11 @@
 from concourse.bass import DstId, RemoteDMATransfer
 
 SCRATCH = {
-    "xs": ("sbuf", [128, 128], "float32"),
+    "xa": ("sbuf", [128, 64], "float32"),
+    "xb": ("sbuf", [128, 64], "float32"),
     "land": ("sbuf", [128, 128], "float32"),
 }
-SEMAPHORES = ["loaded", "sent", "arrived", "stored"]
-CALLS = [(4, 2), (2, 4), (1, 8)]
+SEMAPHORES = ["loaded_a", "loaded_b", "sent_a", "sent_b", "arr_a", "arr_b", "stored_a", "stored_b"]
 
 
 def rank_program(g, core, T, topo):
@@ -16,29 +16,43 @@ def rank_program(g, core, T, topo):
     n = len(grp)
     i = grp.index(rank)
     b = T.x.shape[1] // n
+    hb = n // 2
+    h = i // hb
+    oh = h ^ 1
+    p = i // 2
 
     def blk(j):
         return slice(j * b, (j + 1) * b)
 
-    g.sync.dma_start(T.xs[:, :], T.x[:, :]).then_inc(T.sem.loaded, 16)
-    g.sync.dma_start(T.land[:, blk(i)], T.x[:, blk(i)]).then_inc(T.sem.arrived, 16)
+    def half(k):
+        return slice(k * hb * b, (k + 1) * hb * b)
 
-    g.wait_ge(T.sem.loaded, 16)
-    k = 1
-    total = 0
-    for cnt, eng in CALLS:
+    def call(dests, buf, first, rsem, lsem):
+        eng = 8 // len(dests)
         trs = []
-        for q in range(cnt):
-            j = (i + k) % n
+        for q, j in enumerate(dests):
             rid, pid, _se = topo.addr(T.cores[grp[j]])
             trs.append(RemoteDMATransfer(
                 dst_ids=[DstId(rid=rid, pnc=pid)], dma_engine_mask=((1 << eng) - 1) << (q * eng),
-                remote_sem=T.sem.arrived, src=T.xs[:, blk(j)], dst=T.land[:, blk(i)]))
-            k += 1
-            total += eng
-        g.remote_dma_fused(trs, local_sem=T.sem.sent)
+                remote_sem=rsem, src=buf[:, blk(j - first)], dst=T.land[:, blk(i)]))
+        g.remote_dma_fused(trs, local_sem=lsem)
 
-    g.sync.wait_ge(T.sem.arrived, 16 + total)
-    g.sync.dma_start(T.y[:, :], T.land[:, :]).then_inc(T.sem.stored, 16)
-    g.wait_ge(T.sem.sent, total)
-    g.sync.wait_ge(T.sem.stored, 16)
+    g.sync.dma_start(T.xa[:, :], T.x[:, half(oh)]).then_inc(T.sem.loaded_a, 16)
+    g.scalar.dma_start(T.xb[:, :], T.x[:, half(h)]).then_inc(T.sem.loaded_b, 16)
+
+    g.wait_ge(T.sem.loaded_a, 16)
+    call([oh * hb + q for q in range(hb)], T.xa, oh * hb, T.sem.arr_a, T.sem.sent_a)
+    g.wait_ge(T.sem.loaded_b, 16)
+    call([2 * (p ^ 1), 2 * (p ^ 1) + 1], T.xb, h * hb, T.sem.arr_b, T.sem.sent_b)
+    call([i ^ 1], T.xb, h * hb, T.sem.arr_b, T.sem.sent_b)
+
+    g.sync.wait_ge(T.sem.sent_a, 8)
+    g.sync.dma_start(T.land[:, blk(i)], T.x[:, blk(i)]).then_inc(T.sem.arr_b, 16)
+
+    g.scalar.wait_ge(T.sem.arr_a, 8)
+    g.scalar.dma_start(T.y[:, half(oh)], T.land[:, half(oh)]).then_inc(T.sem.stored_a, 16)
+    g.sync.wait_ge(T.sem.arr_b, 32)
+    g.sync.dma_start(T.y[:, half(h)], T.land[:, half(h)]).then_inc(T.sem.stored_b, 16)
+    g.wait_ge(T.sem.sent_b, 16)
+    g.scalar.wait_ge(T.sem.stored_a, 16)
+    g.sync.wait_ge(T.sem.stored_b, 16)

from concourse.bass import DstId, RemoteDMATransfer

SCRATCH = {
    "xa": ("sbuf", [128, 64], "float32"),
    "xb": ("sbuf", [128, 64], "float32"),
    "land": ("sbuf", [128, 128], "float32"),
}
SEMAPHORES = ["loaded_a", "loaded_b", "sent_a", "sent_b", "arr_a", "arr_b", "stored_a", "stored_b"]


def rank_program(g, core, T, topo):
    rank = T.rank_of(core)
    if rank is None:
        return
    grp = [m for m in T.tables["GROUPS"] if rank in m][0]
    n = len(grp)
    i = grp.index(rank)
    b = T.x.shape[1] // n
    hb = n // 2
    h = i // hb
    oh = h ^ 1
    p = i // 2

    def blk(j):
        return slice(j * b, (j + 1) * b)

    def half(k):
        return slice(k * hb * b, (k + 1) * hb * b)

    def call(dests, buf, first, rsem, lsem):
        eng = 8 // len(dests)
        trs = []
        for q, j in enumerate(dests):
            rid, pid, _se = topo.addr(T.cores[grp[j]])
            trs.append(RemoteDMATransfer(
                dst_ids=[DstId(rid=rid, pnc=pid)], dma_engine_mask=((1 << eng) - 1) << (q * eng),
                remote_sem=rsem, src=buf[:, blk(j - first)], dst=T.land[:, blk(i)]))
        g.remote_dma_fused(trs, local_sem=lsem)

    g.sync.dma_start(T.xa[:, :], T.x[:, half(oh)]).then_inc(T.sem.loaded_a, 16)
    g.scalar.dma_start(T.xb[:, :], T.x[:, half(h)]).then_inc(T.sem.loaded_b, 16)

    g.wait_ge(T.sem.loaded_a, 16)
    call([oh * hb + q for q in range(hb)], T.xa, oh * hb, T.sem.arr_a, T.sem.sent_a)
    g.wait_ge(T.sem.loaded_b, 16)
    call([2 * (p ^ 1), 2 * (p ^ 1) + 1], T.xb, h * hb, T.sem.arr_b, T.sem.sent_b)
    call([i ^ 1], T.xb, h * hb, T.sem.arr_b, T.sem.sent_b)

    g.sync.wait_ge(T.sem.sent_a, 8)
    g.sync.dma_start(T.land[:, blk(i)], T.x[:, blk(i)]).then_inc(T.sem.arr_b, 16)

    g.scalar.wait_ge(T.sem.arr_a, 8)
    g.scalar.dma_start(T.y[:, half(oh)], T.land[:, half(oh)]).then_inc(T.sem.stored_a, 16)
    g.sync.wait_ge(T.sem.arr_b, 32)
    g.sync.dma_start(T.y[:, half(h)], T.land[:, half(h)]).then_inc(T.sem.stored_b, 16)
    g.wait_ge(T.sem.sent_b, 16)
    g.scalar.wait_ge(T.sem.stored_a, 16)
    g.sync.wait_ge(T.sem.stored_b, 16)
